import numpy as np
import ml_dtypes


def mxq(x, axis, fmt="e4m3"):
    dtype, down = {"e4m3": (ml_dtypes.float8_e4m3fn, 7), "e5m2": (ml_dtypes.float8_e5m2, 14)}[fmt]
    v = np.moveaxis(np.asarray(x, np.float32).astype(ml_dtypes.bfloat16).astype(np.float64), axis, -1)
    blocks = v.reshape(v.shape[:-1] + (-1, 32))
    amax = np.abs(blocks).max(-1, keepdims=True)
    byte = np.maximum(np.where(amax > 0, np.frexp(amax)[1] - 1 + 127, 0) - down, 1)
    scale = np.exp2(byte - 127.0)
    codes = (blocks / scale).astype(np.float32).astype(dtype).astype(np.float64)
    return np.moveaxis((codes * scale).reshape(v.shape), -1, axis)


WIDE = False


def mx_kscale(k):
    if not WIDE:
        return np.ones(k)
    levels = np.array([10, -10, 5, -5, 0])
    if k % 512:
        return np.exp2(np.random.permutation(np.resize(levels, k // 32))).repeat(32)
    a = np.empty((k // 512, 16))
    for p in range(k // 512):
        a[p, :8] = np.random.permutation(np.resize(levels, 8))
        for g in range(8):
            far = levels[np.abs(levels - a[p, g]) >= 10]
            a[p, g + 8] = far[np.random.randint(len(far))]
    return np.exp2(a.ravel()).repeat(32)


def f64(x):
    return np.asarray(x).astype(np.float64)


def striped(idx):
    return np.tile(idx.reshape(-1, 16).T, (8, 1)).astype(np.uint16)


def unstriped(offs):
    return offs[:16].T.reshape(-1).astype(np.int64)


def pack_weight(w):
    k, n = w.shape
    w = f64(np.asarray(w, np.float32).astype(ml_dtypes.bfloat16)).reshape(k // 32, 32, n)
    amax = np.abs(w).max(1)
    byte = np.clip(np.where(amax > 0, np.frexp(amax)[1] - 1 + 127 - 7, 1), 1, 254)
    scaled = (w * np.exp2(127.0 - byte)[:, None, :]).reshape(k, n).astype(np.float32)
    words = np.ascontiguousarray(scaled.reshape(k // 512, 128, 4, n).transpose(0, 1, 3, 2)).astype(ml_dtypes.float8_e4m3fn).view(np.uint8)
    return words, np.ascontiguousarray(byte.astype(np.uint8).reshape(k // 512, 16, n))


def unpack_weight(words, scales):
    g, p, n, _ = words.shape
    vals = np.ascontiguousarray(words).view(ml_dtypes.float8_e4m3fn).astype(np.float64) * np.repeat(np.exp2(scales.astype(np.float64) - 127.0), 8, axis=1)[..., None]
    return vals.transpose(0, 1, 3, 2).reshape(g * 512, n)


K, T, S, N, U, D = 512, 2048, 512, 128, 256, 4
P = 2 ** 7


def setup_inputs():
    n = np.random.standard_normal
    s = mx_kscale(K)[:, None]
    packed_xT = pack_weight(n((K, T)) * s)
    return {
        "x_words": packed_xT[0],
        "x_scales": packed_xT[1],
        "w1": (n((K, N)) / np.sqrt(K) / s).astype(np.float32),
        "wgt": (np.tile(np.random.uniform(0.1, 0.4, (D, 1, U)), (1, P, 1))).astype(np.float32),
        "old": (n((N, S))).astype(np.float32),
        "vel": (n((N, U))).astype(np.float32),
        "offs": striped(np.random.permutation(T)[:S]),
        "cor1": striped(np.random.randint(0, S, U)),
        "cor2": striped(np.random.randint(0, S, U)),
        "cor3": striped(np.random.randint(0, S, U)),
        "cor4": striped(np.random.randint(0, S, U)),
    }


def reference(x_words, x_scales, w1, wgt, old, vel, offs, cor1, cor2, cor3, cor4):
    xq = unpack_weight(x_words, x_scales)[:, unstriped(offs)]
    y = mxq(f64(w1), 0, "e4m3").T @ xq
    g0 = y[:, unstriped(cor1)]
    g1 = y[:, unstriped(cor2)]
    g2 = y[:, unstriped(cor3)]
    g3 = y[:, unstriped(cor4)]
    pic = g0 * f64(wgt)[0, :1] + g1 * f64(wgt)[1, :1] + g2 * f64(wgt)[2, :1] + g3 * f64(wgt)[3, :1]
    tr = f64(vel) + pic - (f64(old)[:, unstriped(cor1)] * f64(wgt)[0, :1] + f64(old)[:, unstriped(cor2)] * f64(wgt)[1, :1] + f64(old)[:, unstriped(cor3)] * f64(wgt)[2, :1] + f64(old)[:, unstriped(cor4)] * f64(wgt)[3, :1])
    return np.minimum(np.maximum(tr, np.minimum(np.minimum(np.minimum(g0, g1), g2), g3)), np.maximum(np.maximum(np.maximum(g0, g1), g2), g3))

@@ -1,0 +1,134 @@
+from contextlib import ExitStack
+
+import concourse.mybir as mybir
+from concourse.masks import make_identity
+
+F32 = mybir.dt.float32
+BF16 = mybir.dt.bfloat16
+I32 = mybir.dt.int32
+U32 = mybir.dt.uint32
+U16 = mybir.dt.uint16
+U8 = mybir.dt.uint8
+FP8X4 = mybir.dt.float8_e4m3fn_x4
+ALU = mybir.AluOpType
+COPY = mybir.ActivationFunctionType.Copy
+
+P = 128
+K, T, S, N, U, D = 512, 2048, 512, 128, 256, 4
+PIECES = ((0, 256), (256, 384), (384, 512))
+FLOPS = 2 * K * N * S
+
+
+def tile_picked_yflip_clamp_p_kernel(tc, x_words, x_scales, w1, wgt, old, vel, offs, cor1, cor2, cor3, cor4, out):
+    nc = tc.nc
+    with ExitStack() as ctx:
+        sb = ctx.enter_context(tc.tile_pool(name="sb", bufs=1))
+        ps = ctx.enter_context(tc.psum_pool(name="ps", bufs=1))
+
+        cell_list = sb.tile([P, S // 16], U16, name="cell_list")
+        corner = [sb.tile([P, U // 16], U16, name=f"corner{d}") for d in range(D)]
+        words = sb.tile([P, T], U32, name="words", align_bytes=64)
+        scales = sb.tile([P, T], U8, name="scales", align_bytes=64)
+        w_raw = sb.tile([P, 4, N], F32, name="w_raw")
+        old_sb = sb.tile([P, S], F32, name="old_sb")
+        vel_sb = sb.tile([P, U], F32, name="vel_sb")
+        wgt_rows = sb.tile([P, U], F32, name="wgt_rows")
+        ident = sb.tile([P, P], F32, name="ident")
+
+        nc.vector.memset(scales[:].bitcast(I32), 0)
+        nc.vector.memset(wgt_rows[:], 0.0)
+
+        nc.scalar.dma_start(out=w_raw[:], in_=w1.rearrange("(p j) m -> p j m", j=4))
+        nc.scalar.dma_start(out=old_sb[:], in_=old)
+        nc.scalar.dma_start(out=words[:].bitcast(I32), in_=x_words[0].rearrange("p n t -> p (n t)").bitcast(I32))
+        nc.sync.dma_start(cell_list[:], offs)
+        for q in range(4):
+            nc.sync.dma_start(
+                out=scales[32 * q : 32 * q + 4, :].bitcast(I32),
+                in_=x_scales[0, 4 * q : 4 * q + 4, :].bitcast(I32),
+            )
+        for tile, lst in zip(corner, (cor1, cor2, cor3, cor4)):
+            nc.sync.dma_start(tile[:], lst)
+        nc.gpsimd.dma_start(out=vel_sb[:], in_=vel)
+        nc.gpsimd.dma_start(out=wgt_rows[0:D, :], in_=wgt[:, 0, :])
+        make_identity(nc, ident[:])
+
+        w_bf = sb.tile([P, N, 4], BF16, name="w_bf", align_bytes=64)
+        w_codes = sb.tile([P, N], U32, name="w_codes", align_bytes=64)
+        w_scales = sb.tile([P, N], U8, name="w_scales", align_bytes=64)
+        nc.vector.tensor_copy(out=w_bf[:], in_=w_raw[:].rearrange("p j m -> p m j"))
+        picked_scales = sb.tile([P, S], U8, name="picked_scales", align_bytes=64)
+        nc.vector.tensor_copy(out=picked_scales[:], in_=scales[:].indirect(cell_list[:]))
+        nc.vector.quantize_mx(out=w_codes[:].bitcast(FP8X4), scales=w_scales[:], in_=w_bf[:].rearrange("p m j -> p (m j)"))
+
+        diff_t = [ps.tile([P, 4, P], F32, name=f"diff_t{d}") for d in range(D)]
+        neg_old = sb.tile([P, D, U], F32, name="neg_old")
+        for d in range(D):
+            nc.scalar.activation(out=neg_old[:, d, :], in_=old_sb[:].indirect(corner[d][:]), func=COPY, scale=-1.0)
+            for h in range(2):
+                nc.tensor.matmul(diff_t[d][:, h, :], lhsT=neg_old[:, d, h * P : (h + 1) * P], rhs=ident[:], is_transpose=True, start=(h == 0), stop=False)
+
+        turned = ps.tile([P, 4, P], F32, name="turned", tag="shared")
+        for h in range(2):
+            nc.tensor.transpose(turned[:, h, :], wgt_rows[:, h * P : (h + 1) * P], ident[:])
+            nc.tensor.transpose(turned[:, 2 + h, :], vel_sb[:, h * P : (h + 1) * P], ident[:])
+        wgt_t = sb.tile([P, 2, D], F32, name="wgt_t")
+        vel_t = sb.tile([P, 2, P], F32, name="vel_t")
+        nc.scalar.copy(out=wgt_t[:], in_=turned[:, 0:2, 0:D])
+        nc.scalar.copy(out=vel_t[:], in_=turned[:, 2:4, :])
+        trial = ps.tile([P, 4, P], F32, name="trial", tag="shared")
+        for h in range(2):
+            nc.tensor.matmul(trial[:, h, :], lhsT=vel_t[:, h, :], rhs=ident[:], is_transpose=True, start=(h == 0), stop=False)
+
+        picked_words = sb.tile([P, S], U32, name="picked_words", align_bytes=64)
+        y = sb.tile([P, S], F32, name="y")
+        banks = []
+        for i, (a, b) in enumerate(PIECES):
+            nc.vector.tensor_copy(out=picked_words[:, a:b], in_=words[:].indirect(cell_list[:, a // 16 : b // 16]))
+            bank = ps.tile([P, S], F32, name=f"y_bank{i}")
+            nc.tensor.matmul_mx(
+                out=bank[:, 0 : b - a],
+                lhsT=w_codes[:].bitcast(FP8X4),
+                lhsT_scale=w_scales[:],
+                rhs=picked_words[:, a:b].bitcast(FP8X4),
+                rhs_scale=picked_scales[:, a:b],
+                start=True,
+                stop=True,
+            )
+            banks.append(bank)
+        for bank, (a, b) in zip(banks, PIECES):
+            nc.vector.tensor_copy(out=y[:, a:b], in_=bank[:, 0 : b - a])
+
+        g_vec = sb.tile([P, 2, U], F32, name="g_vec")
+        g_act = sb.tile([P, 2, U], F32, name="g_act")
+        g = [g_vec[:, 0, :], g_vec[:, 1, :], g_act[:, 0, :], g_act[:, 1, :]]
+        order = (0, 2, 1, 3)
+        for d in order:
+            if d < 2:
+                nc.vector.tensor_copy(out=g[d], in_=y[:].indirect(corner[d][:]))
+            else:
+                nc.scalar.activation(out=g[d], in_=y[:].indirect(corner[d][:]), func=COPY)
+            for h in range(2):
+                nc.tensor.matmul(diff_t[d][:, h, :], lhsT=g[d][:, h * P : (h + 1) * P], rhs=ident[:], is_transpose=True, start=False, stop=(h == 1))
+        term_t = sb.tile([P, D, 2, P], F32, name="term_t")
+        for d in order:
+            for h in range(2):
+                nc.scalar.activation(out=term_t[:, d, h, :], in_=diff_t[d][:, h, :], func=COPY, scale=wgt_t[:, h, d : d + 1])
+                nc.tensor.matmul(trial[:, h, :], lhsT=term_t[:, d, h, :], rhs=ident[:], is_transpose=True, start=False, stop=(d == order[-1] and h == 1))
+
+        low2 = sb.tile([P, 2, U], F32, name="low2")
+        high2 = sb.tile([P, 2, U], F32, name="high2")
+        low = sb.tile([P, U], F32, name="low")
+        high = sb.tile([P, U], F32, name="high")
+        nc.vector.tensor_tensor(out=low2[:], in0=g_vec[:], in1=g_act[:], op=ALU.min)
+        nc.vector.tensor_tensor(out=high2[:], in0=g_vec[:], in1=g_act[:], op=ALU.max)
+        nc.vector.tensor_tensor(out=low[:], in0=low2[:, 0, :], in1=low2[:, 1, :], op=ALU.min)
+        nc.vector.tensor_tensor(out=high[:], in0=high2[:, 0, :], in1=high2[:, 1, :], op=ALU.max)
+        raised = sb.tile([P, U], F32, name="raised")
+        result = sb.tile([P, U], F32, name="result")
+        for h in range(2):
+            nc.vector.tensor_tensor(out=raised[:, h * P : (h + 1) * P], in0=trial[:, h, :], in1=low[:, h * P : (h + 1) * P], op=ALU.max)
+        for h, queue in enumerate((nc.sync, nc.scalar)):
+            cols = slice(h * P, (h + 1) * P)
+            nc.vector.tensor_tensor(out=result[:, cols], in0=raised[:, cols], in1=high[:, cols], op=ALU.min)
+            queue.dma_start(out=out[:, cols], in_=result[:, cols])

@@ -32,60 +32,46 @@ def tile_picked_yflip_clamp_p_kernel(tc, x_words, x_scales, w1, wgt, old, vel, o
         w_raw = sb.tile([P, 4, N], F32, name="w_raw")
         old_sb = sb.tile([P, S], F32, name="old_sb")
         vel_sb = sb.tile([P, U], F32, name="vel_sb")
-        wgt_rows = sb.tile([P, U], F32, name="wgt_rows")
+        wgt_rows = sb.tile([P, P], F32, name="wgt_rows")
         ident = sb.tile([P, P], F32, name="ident")
 
-        nc.vector.memset(scales[:].bitcast(I32), 0)
-        nc.vector.memset(wgt_rows[:], 0.0)
+        zero_view = scales[:].bitcast(I32)
+        nc.vector.memset(zero_view[:, 0 : T // 8], 0)
+        nc.gpsimd.memset(zero_view[:, T // 8 : T // 4], 0)
+        make_identity(nc, ident[:])
 
-        nc.scalar.dma_start(out=w_raw[:], in_=w1.rearrange("(p j) m -> p j m", j=4))
-        nc.scalar.dma_start(out=old_sb[:], in_=old)
-        nc.scalar.dma_start(out=words[:].bitcast(I32), in_=x_words[0].rearrange("p n t -> p (n t)").bitcast(I32))
-        nc.sync.dma_start(cell_list[:], offs)
-        for q in range(4):
-            nc.sync.dma_start(
+        def load_scales(queue, q):
+            queue.dma_start(
                 out=scales[32 * q : 32 * q + 4, :].bitcast(I32),
                 in_=x_scales[0, 4 * q : 4 * q + 4, :].bitcast(I32),
             )
+
+        nc.scalar.dma_start(out=w_raw[:], in_=w1.rearrange("(p j) m -> p j m", j=4))
+        for q in range(4):
+            load_scales(nc.sync, q)
+        nc.sync.dma_start(cell_list[:], offs)
+        nc.sync.dma_start(out=old_sb[:], in_=old)
         for tile, lst in zip(corner, (cor1, cor2, cor3, cor4)):
             nc.sync.dma_start(tile[:], lst)
-        nc.gpsimd.dma_start(out=vel_sb[:], in_=vel)
-        nc.gpsimd.dma_start(out=wgt_rows[0:D, :], in_=wgt[:, 0, :])
-        make_identity(nc, ident[:])
+        nc.gpsimd.memset(wgt_rows[:], 0.0)
+        nc.sync.dma_start(out=wgt_rows[0 : 2 * D, :], in_=wgt.rearrange("d p (h c) -> (d p h) c", h=2)[0 : 2 * D * P : P + 1, :])
+        nc.sync.dma_start(out=vel_sb[:], in_=vel)
+        nc.sync.dma_start(out=words[:].bitcast(I32), in_=x_words[0].rearrange("p n t -> p (n t)").bitcast(I32))
 
         w_bf = sb.tile([P, N, 4], BF16, name="w_bf", align_bytes=64)
         w_codes = sb.tile([P, N], U32, name="w_codes", align_bytes=64)
         w_scales = sb.tile([P, N], U8, name="w_scales", align_bytes=64)
-        nc.vector.tensor_copy(out=w_bf[:], in_=w_raw[:].rearrange("p j m -> p m j"))
+        nc.scalar.activation(out=w_bf[:], in_=w_raw[:].rearrange("p j m -> p m j"), func=COPY)
         picked_scales = sb.tile([P, S], U8, name="picked_scales", align_bytes=64)
         nc.vector.tensor_copy(out=picked_scales[:], in_=scales[:].indirect(cell_list[:]))
         nc.vector.quantize_mx(out=w_codes[:].bitcast(FP8X4), scales=w_scales[:], in_=w_bf[:].rearrange("p m j -> p (m j)"))
-
-        diff_t = [ps.tile([P, 4, P], F32, name=f"diff_t{d}") for d in range(D)]
-        neg_old = sb.tile([P, D, U], F32, name="neg_old")
-        for d in range(D):
-            nc.scalar.activation(out=neg_old[:, d, :], in_=old_sb[:].indirect(corner[d][:]), func=COPY, scale=-1.0)
-            for h in range(2):
-                nc.tensor.matmul(diff_t[d][:, h, :], lhsT=neg_old[:, d, h * P : (h + 1) * P], rhs=ident[:], is_transpose=True, start=(h == 0), stop=False)
-
-        turned = ps.tile([P, 4, P], F32, name="turned", tag="shared")
-        for h in range(2):
-            nc.tensor.transpose(turned[:, h, :], wgt_rows[:, h * P : (h + 1) * P], ident[:])
-            nc.tensor.transpose(turned[:, 2 + h, :], vel_sb[:, h * P : (h + 1) * P], ident[:])
-        wgt_t = sb.tile([P, 2, D], F32, name="wgt_t")
-        vel_t = sb.tile([P, 2, P], F32, name="vel_t")
-        nc.scalar.copy(out=wgt_t[:], in_=turned[:, 0:2, 0:D])
-        nc.scalar.copy(out=vel_t[:], in_=turned[:, 2:4, :])
-        trial = ps.tile([P, 4, P], F32, name="trial", tag="shared")
-        for h in range(2):
-            nc.tensor.matmul(trial[:, h, :], lhsT=vel_t[:, h, :], rhs=ident[:], is_transpose=True, start=(h == 0), stop=False)
 
         picked_words = sb.tile([P, S], U32, name="picked_words", align_bytes=64)
         y = sb.tile([P, S], F32, name="y")
         banks = []
         for i, (a, b) in enumerate(PIECES):
             nc.vector.tensor_copy(out=picked_words[:, a:b], in_=words[:].indirect(cell_list[:, a // 16 : b // 16]))
-            bank = ps.tile([P, S], F32, name=f"y_bank{i}")
+            bank = ps.tile([P, S], F32, name=f"y_bank{i}", tag=f"y_bank{i}")
             nc.tensor.matmul_mx(
                 out=bank[:, 0 : b - a],
                 lhsT=w_codes[:].bitcast(FP8X4),
@@ -99,6 +85,26 @@ def tile_picked_yflip_clamp_p_kernel(tc, x_words, x_scales, w1, wgt, old, vel, o
         for bank, (a, b) in zip(banks, PIECES):
             nc.vector.tensor_copy(out=y[:, a:b], in_=bank[:, 0 : b - a])
 
+        diff_t = [ps.tile([P, 4, P], F32, name=f"diff_t{d}") for d in range(D)]
+        neg_pair = [sb.tile([P, 2, U], F32, name=f"neg_pair{i}", tag=f"neg_pair{i}") for i in range(2)]
+        neg_old = [neg_pair[d // 2][:, d % 2, :] for d in range(D)]
+        for d in range(D):
+            nc.scalar.activation(out=neg_old[d], in_=old_sb[:].indirect(corner[d][:]), func=COPY, scale=-1.0)
+            for h in range(2):
+                nc.tensor.matmul(diff_t[d][:, h, :], lhsT=neg_old[d][:, h * P : (h + 1) * P], rhs=ident[:], is_transpose=True, start=(h == 0), stop=False)
+
+        turned = ps.tile([P, 4, P], F32, name="turned", tag="shared")
+        nc.tensor.transpose(turned[:, 0, :], wgt_rows[:], ident[:])
+        for h in range(2):
+            nc.tensor.transpose(turned[:, 2 + h, :], vel_sb[:, h * P : (h + 1) * P], ident[:])
+        wgt_t = sb.tile([P, 2 * D], F32, name="wgt_t")
+        vel_t = sb.tile([P, 2, P], F32, name="vel_t")
+        nc.scalar.copy(out=wgt_t[:], in_=turned[:, 0, 0 : 2 * D])
+        nc.scalar.copy(out=vel_t[:], in_=turned[:, 2:4, :])
+        trial = ps.tile([P, 4, P], F32, name="trial", tag="shared")
+        for h in range(2):
+            nc.tensor.matmul(trial[:, h, :], lhsT=vel_t[:, h, :], rhs=ident[:], is_transpose=True, start=(h == 0), stop=False)
+
         g_vec = sb.tile([P, 2, U], F32, name="g_vec")
         g_act = sb.tile([P, 2, U], F32, name="g_act")
         g = [g_vec[:, 0, :], g_vec[:, 1, :], g_act[:, 0, :], g_act[:, 1, :]]
@@ -110,11 +116,12 @@ def tile_picked_yflip_clamp_p_kernel(tc, x_words, x_scales, w1, wgt, old, vel, o
                 nc.scalar.activation(out=g[d], in_=y[:].indirect(corner[d][:]), func=COPY)
             for h in range(2):
                 nc.tensor.matmul(diff_t[d][:, h, :], lhsT=g[d][:, h * P : (h + 1) * P], rhs=ident[:], is_transpose=True, start=False, stop=(h == 1))
-        term_t = sb.tile([P, D, 2, P], F32, name="term_t")
+
+        term_t = [[sb.tile([P, P], F32, name=f"term_t{d}{h}") for h in range(2)] for d in range(D)]
         for d in order:
             for h in range(2):
-                nc.scalar.activation(out=term_t[:, d, h, :], in_=diff_t[d][:, h, :], func=COPY, scale=wgt_t[:, h, d : d + 1])
-                nc.tensor.matmul(trial[:, h, :], lhsT=term_t[:, d, h, :], rhs=ident[:], is_transpose=True, start=False, stop=(d == order[-1] and h == 1))
+                nc.scalar.activation(out=term_t[d][h][:], in_=diff_t[d][:, h, :], func=COPY, scale=wgt_t[:, 2 * d + h : 2 * d + h + 1])
+                nc.tensor.matmul(trial[:, h, :], lhsT=term_t[d][h][:], rhs=ident[:], is_transpose=True, start=False, stop=(d == order[-1] and h == 1))
 
         low2 = sb.tile([P, 2, U], F32, name="low2")
         high2 = sb.tile([P, 2, U], F32, name="high2")

@@ -36,8 +36,8 @@ def tile_picked_yflip_clamp_p_kernel(tc, x_words, x_scales, w1, wgt, old, vel, o
         ident = sb.tile([P, P], F32, name="ident")
 
         zero_view = scales[:].bitcast(I32)
-        nc.vector.memset(zero_view[:, 0 : T // 8], 0)
-        nc.gpsimd.memset(zero_view[:, T // 8 : T // 4], 0)
+        nc.vector.memset(zero_view[:, 0:320], 0)
+        nc.gpsimd.memset(zero_view[:, 320 : T // 4], 0)
         make_identity(nc, ident[:])
 
         def load_scales(queue, q):
@@ -50,13 +50,13 @@ def tile_picked_yflip_clamp_p_kernel(tc, x_words, x_scales, w1, wgt, old, vel, o
         for q in range(4):
             load_scales(nc.sync, q)
         nc.sync.dma_start(cell_list[:], offs)
-        nc.sync.dma_start(out=old_sb[:], in_=old)
-        for tile, lst in zip(corner, (cor1, cor2, cor3, cor4)):
-            nc.sync.dma_start(tile[:], lst)
         nc.gpsimd.memset(wgt_rows[:], 0.0)
         nc.sync.dma_start(out=wgt_rows[0 : 2 * D, :], in_=wgt.rearrange("d p (h c) -> (d p h) c", h=2)[0 : 2 * D * P : P + 1, :])
-        nc.sync.dma_start(out=vel_sb[:], in_=vel)
         nc.sync.dma_start(out=words[:].bitcast(I32), in_=x_words[0].rearrange("p n t -> p (n t)").bitcast(I32))
+        nc.sync.dma_start(out=old_sb[:], in_=old)
+        nc.sync.dma_start(out=vel_sb[:], in_=vel)
+        for tile, lst in zip(corner, (cor1, cor2, cor3, cor4)):
+            nc.sync.dma_start(tile[:], lst)
 
         w_bf = sb.tile([P, N, 4], BF16, name="w_bf", align_bytes=64)
         w_codes = sb.tile([P, N], U32, name="w_codes", align_bytes=64)
@@ -66,12 +66,22 @@ def tile_picked_yflip_clamp_p_kernel(tc, x_words, x_scales, w1, wgt, old, vel, o
         nc.vector.tensor_copy(out=picked_scales[:], in_=scales[:].indirect(cell_list[:]))
         nc.vector.quantize_mx(out=w_codes[:].bitcast(FP8X4), scales=w_scales[:], in_=w_bf[:].rearrange("p m j -> p (m j)"))
 
+        def turn(dst, src, start, stop):
+            nc.tensor.matmul(dst, lhsT=src, rhs=ident[:], is_transpose=True, start=start, stop=stop)
+
+        halves = [slice(h * P, (h + 1) * P) for h in range(2)]
+        wgt_turned = ps.tile([P, 4, P], F32, name="wgt_turned", tag="shared")
+        turn(wgt_turned[:, 0, :], wgt_rows[:], True, True)
+        wgt_t = sb.tile([P, 2 * D], F32, name="wgt_t")
+        nc.scalar.copy(out=wgt_t[:], in_=wgt_turned[:, 0, 0 : 2 * D])
+
         picked_words = sb.tile([P, S], U32, name="picked_words", align_bytes=64)
         y = sb.tile([P, S], F32, name="y")
+        change = sb.tile([P, S], F32, name="change", tag="change_then_terms")
         banks = []
         for i, (a, b) in enumerate(PIECES):
             nc.vector.tensor_copy(out=picked_words[:, a:b], in_=words[:].indirect(cell_list[:, a // 16 : b // 16]))
-            bank = ps.tile([P, S], F32, name=f"y_bank{i}", tag=f"y_bank{i}")
+            bank = ps.tile([P, S], F32, name=f"y_bank{i}")
             nc.tensor.matmul_mx(
                 out=bank[:, 0 : b - a],
                 lhsT=w_codes[:].bitcast(FP8X4),
@@ -83,59 +93,49 @@ def tile_picked_yflip_clamp_p_kernel(tc, x_words, x_scales, w1, wgt, old, vel, o
             )
             banks.append(bank)
         for bank, (a, b) in zip(banks, PIECES):
-            nc.vector.tensor_copy(out=y[:, a:b], in_=bank[:, 0 : b - a])
+            nc.scalar.copy(out=y[:, a:b], in_=bank[:, 0 : b - a])
+            nc.vector.tensor_tensor(out=change[:, a:b], in0=bank[:, 0 : b - a], in1=old_sb[:, a:b], op=ALU.subtract)
 
-        diff_t = [ps.tile([P, 4, P], F32, name=f"diff_t{d}") for d in range(D)]
-        neg_pair = [sb.tile([P, 2, U], F32, name=f"neg_pair{i}", tag=f"neg_pair{i}") for i in range(2)]
-        neg_old = [neg_pair[d // 2][:, d % 2, :] for d in range(D)]
-        for d in range(D):
-            nc.scalar.activation(out=neg_old[d], in_=old_sb[:].indirect(corner[d][:]), func=COPY, scale=-1.0)
-            for h in range(2):
-                nc.tensor.matmul(diff_t[d][:, h, :], lhsT=neg_old[d][:, h * P : (h + 1) * P], rhs=ident[:], is_transpose=True, start=(h == 0), stop=False)
-
-        turned = ps.tile([P, 4, P], F32, name="turned", tag="shared")
-        nc.tensor.transpose(turned[:, 0, :], wgt_rows[:], ident[:])
+        vel_turned = ps.tile([P, 4, P], F32, name="vel_turned", tag="shared")
         for h in range(2):
-            nc.tensor.transpose(turned[:, 2 + h, :], vel_sb[:, h * P : (h + 1) * P], ident[:])
-        wgt_t = sb.tile([P, 2 * D], F32, name="wgt_t")
+            turn(vel_turned[:, h, :], vel_sb[:, halves[h]], True, True)
         vel_t = sb.tile([P, 2, P], F32, name="vel_t")
-        nc.scalar.copy(out=wgt_t[:], in_=turned[:, 0, 0 : 2 * D])
-        nc.scalar.copy(out=vel_t[:], in_=turned[:, 2:4, :])
+        nc.scalar.copy(out=vel_t[:], in_=vel_turned[:, 0:2, :])
         trial = ps.tile([P, 4, P], F32, name="trial", tag="shared")
         for h in range(2):
-            nc.tensor.matmul(trial[:, h, :], lhsT=vel_t[:, h, :], rhs=ident[:], is_transpose=True, start=(h == 0), stop=False)
+            turn(trial[:, h, :], vel_t[:, h, :], h == 0, False)
 
-        g_vec = sb.tile([P, 2, U], F32, name="g_vec")
-        g_act = sb.tile([P, 2, U], F32, name="g_act")
-        g = [g_vec[:, 0, :], g_vec[:, 1, :], g_act[:, 0, :], g_act[:, 1, :]]
-        order = (0, 2, 1, 3)
-        for d in order:
-            if d < 2:
-                nc.vector.tensor_copy(out=g[d], in_=y[:].indirect(corner[d][:]))
+        g = sb.tile([P, D, U], F32, name="g")
+        change_at = [sb.tile([P, U], F32, name=f"change_at{d}") for d in range(D)]
+        change_t = [ps.tile([P, 4, P], F32, name=f"change_t{d}") for d in range(D)]
+        for d in range(D):
+            if d < D - 1:
+                nc.scalar.activation(out=change_at[d][:], in_=change[:].indirect(corner[d][:]), func=COPY)
             else:
-                nc.scalar.activation(out=g[d], in_=y[:].indirect(corner[d][:]), func=COPY)
+                nc.scalar.activation(out=change_at[d][:, halves[0]], in_=change[:].indirect(corner[d][:, 0 : P // 16]), func=COPY)
+                nc.vector.tensor_copy(out=change_at[d][:, halves[1]], in_=change[:].indirect(corner[d][:, P // 16 : U // 16]))
+            nc.vector.tensor_copy(out=g[:, d, :], in_=y[:].indirect(corner[d][:]))
             for h in range(2):
-                nc.tensor.matmul(diff_t[d][:, h, :], lhsT=g[d][:, h * P : (h + 1) * P], rhs=ident[:], is_transpose=True, start=False, stop=(h == 1))
+                turn(change_t[d][:, h, :], change_at[d][:, halves[h]], True, True)
 
-        term_t = [[sb.tile([P, P], F32, name=f"term_t{d}{h}") for h in range(2)] for d in range(D)]
-        for d in order:
+        term_t = sb.tile([P, D, 2, P], F32, name="term_t", tag="change_then_terms")
+        for d in range(D):
             for h in range(2):
-                nc.scalar.activation(out=term_t[d][h][:], in_=diff_t[d][:, h, :], func=COPY, scale=wgt_t[:, 2 * d + h : 2 * d + h + 1])
-                nc.tensor.matmul(trial[:, h, :], lhsT=term_t[d][h][:], rhs=ident[:], is_transpose=True, start=False, stop=(d == order[-1] and h == 1))
+                nc.scalar.activation(out=term_t[:, d, h, :], in_=change_t[d][:, h, :], func=COPY, scale=wgt_t[:, 2 * d + h : 2 * d + h + 1])
+                turn(trial[:, h, :], term_t[:, d, h, :], False, d == D - 1 and h == 1)
 
         low2 = sb.tile([P, 2, U], F32, name="low2")
         high2 = sb.tile([P, 2, U], F32, name="high2")
         low = sb.tile([P, U], F32, name="low")
         high = sb.tile([P, U], F32, name="high")
-        nc.vector.tensor_tensor(out=low2[:], in0=g_vec[:], in1=g_act[:], op=ALU.min)
-        nc.vector.tensor_tensor(out=high2[:], in0=g_vec[:], in1=g_act[:], op=ALU.max)
+        nc.vector.tensor_tensor(out=low2[:], in0=g[:, 0:2, :], in1=g[:, 2:4, :], op=ALU.min)
+        nc.vector.tensor_tensor(out=high2[:], in0=g[:, 0:2, :], in1=g[:, 2:4, :], op=ALU.max)
         nc.vector.tensor_tensor(out=low[:], in0=low2[:, 0, :], in1=low2[:, 1, :], op=ALU.min)
         nc.vector.tensor_tensor(out=high[:], in0=high2[:, 0, :], in1=high2[:, 1, :], op=ALU.max)
         raised = sb.tile([P, U], F32, name="raised")
         result = sb.tile([P, U], F32, name="result")
         for h in range(2):
-            nc.vector.tensor_tensor(out=raised[:, h * P : (h + 1) * P], in0=trial[:, h, :], in1=low[:, h * P : (h + 1) * P], op=ALU.max)
+            nc.vector.tensor_tensor(out=raised[:, halves[h]], in0=trial[:, h, :], in1=low[:, halves[h]], op=ALU.max)
         for h, queue in enumerate((nc.sync, nc.scalar)):
-            cols = slice(h * P, (h + 1) * P)
-            nc.vector.tensor_tensor(out=result[:, cols], in0=raised[:, cols], in1=high[:, cols], op=ALU.min)
-            queue.dma_start(out=out[:, cols], in_=result[:, cols])
+            nc.vector.tensor_tensor(out=result[:, halves[h]], in0=raised[:, halves[h]], in1=high[:, halves[h]], op=ALU.min)
+            queue.dma_start(out=out[:, halves[h]], in_=result[:, halves[h]])

@@ -50,10 +50,10 @@ def tile_picked_yflip_clamp_p_kernel(tc, x_words, x_scales, w1, wgt, old, vel, o
         for q in range(4):
             load_scales(nc.sync, q)
         nc.sync.dma_start(cell_list[:], offs)
-        nc.gpsimd.memset(wgt_rows[:], 0.0)
-        nc.sync.dma_start(out=wgt_rows[0 : 2 * D, :], in_=wgt.rearrange("d p (h c) -> (d p h) c", h=2)[0 : 2 * D * P : P + 1, :])
         nc.sync.dma_start(out=words[:].bitcast(I32), in_=x_words[0].rearrange("p n t -> p (n t)").bitcast(I32))
         nc.sync.dma_start(out=old_sb[:], in_=old)
+        nc.gpsimd.memset(wgt_rows[:], 0.0)
+        nc.sync.dma_start(out=wgt_rows[0 : 2 * D, :], in_=wgt.rearrange("d p (h c) -> (d p h) c", h=2)[0 : 2 * D * P : P + 1, :])
         nc.sync.dma_start(out=vel_sb[:], in_=vel)
         for tile, lst in zip(corner, (cor1, cor2, cor3, cor4)):
             nc.sync.dma_start(tile[:], lst)
@@ -70,11 +70,6 @@ def tile_picked_yflip_clamp_p_kernel(tc, x_words, x_scales, w1, wgt, old, vel, o
             nc.tensor.matmul(dst, lhsT=src, rhs=ident[:], is_transpose=True, start=start, stop=stop)
 
         halves = [slice(h * P, (h + 1) * P) for h in range(2)]
-        wgt_turned = ps.tile([P, 4, P], F32, name="wgt_turned", tag="shared")
-        turn(wgt_turned[:, 0, :], wgt_rows[:], True, True)
-        wgt_t = sb.tile([P, 2 * D], F32, name="wgt_t")
-        nc.scalar.copy(out=wgt_t[:], in_=wgt_turned[:, 0, 0 : 2 * D])
-
         picked_words = sb.tile([P, S], U32, name="picked_words", align_bytes=64)
         y = sb.tile([P, S], F32, name="y")
         change = sb.tile([P, S], F32, name="change", tag="change_then_terms")
@@ -96,11 +91,14 @@ def tile_picked_yflip_clamp_p_kernel(tc, x_words, x_scales, w1, wgt, old, vel, o
             nc.scalar.copy(out=y[:, a:b], in_=bank[:, 0 : b - a])
             nc.vector.tensor_tensor(out=change[:, a:b], in0=bank[:, 0 : b - a], in1=old_sb[:, a:b], op=ALU.subtract)
 
-        vel_turned = ps.tile([P, 4, P], F32, name="vel_turned", tag="shared")
+        turned = ps.tile([P, 4, P], F32, name="turned", tag="shared")
+        turn(turned[:, 0, :], wgt_rows[:], True, True)
         for h in range(2):
-            turn(vel_turned[:, h, :], vel_sb[:, halves[h]], True, True)
+            turn(turned[:, 2 + h, :], vel_sb[:, halves[h]], True, True)
+        wgt_t = sb.tile([P, 2 * D], F32, name="wgt_t")
         vel_t = sb.tile([P, 2, P], F32, name="vel_t")
-        nc.scalar.copy(out=vel_t[:], in_=vel_turned[:, 0:2, :])
+        nc.scalar.copy(out=wgt_t[:], in_=turned[:, 0, 0 : 2 * D])
+        nc.scalar.copy(out=vel_t[:], in_=turned[:, 2:4, :])
         trial = ps.tile([P, 4, P], F32, name="trial", tag="shared")
         for h in range(2):
             turn(trial[:, h, :], vel_t[:, h, :], h == 0, False)

from contextlib import ExitStack

import concourse.mybir as mybir
from concourse.masks import make_identity

F32 = mybir.dt.float32
BF16 = mybir.dt.bfloat16
I32 = mybir.dt.int32
U32 = mybir.dt.uint32
U16 = mybir.dt.uint16
U8 = mybir.dt.uint8
FP8X4 = mybir.dt.float8_e4m3fn_x4
ALU = mybir.AluOpType
COPY = mybir.ActivationFunctionType.Copy

P = 128
K, T, S, N, U, D = 512, 2048, 512, 128, 256, 4
PIECES = ((0, 256), (256, 384), (384, 512))
FLOPS = 2 * K * N * S


def tile_picked_yflip_clamp_p_kernel(tc, x_words, x_scales, w1, wgt, old, vel, offs, cor1, cor2, cor3, cor4, out):
    nc = tc.nc
    with ExitStack() as ctx:
        sb = ctx.enter_context(tc.tile_pool(name="sb", bufs=1))
        ps = ctx.enter_context(tc.psum_pool(name="ps", bufs=1))

        cell_list = sb.tile([P, S // 16], U16, name="cell_list")
        corner = [sb.tile([P, U // 16], U16, name=f"corner{d}") for d in range(D)]
        words = sb.tile([P, T], U32, name="words", align_bytes=64)
        scales = sb.tile([P, T], U8, name="scales", align_bytes=64)
        w_raw = sb.tile([P, 4, N], F32, name="w_raw")
        old_sb = sb.tile([P, S], F32, name="old_sb")
        vel_sb = sb.tile([P, U], F32, name="vel_sb")
        wgt_rows = sb.tile([P, P], F32, name="wgt_rows")
        ident = sb.tile([P, P], F32, name="ident")

        zero_view = scales[:].bitcast(I32)
        nc.vector.memset(zero_view[:, 0:320], 0)
        nc.gpsimd.memset(zero_view[:, 320 : T // 4], 0)
        make_identity(nc, ident[:])

        def load_scales(queue, q):
            queue.dma_start(
                out=scales[32 * q : 32 * q + 4, :].bitcast(I32),
                in_=x_scales[0, 4 * q : 4 * q + 4, :].bitcast(I32),
            )

        nc.scalar.dma_start(out=w_raw[:], in_=w1.rearrange("(p j) m -> p j m", j=4))
        for q in range(4):
            load_scales(nc.sync, q)
        nc.sync.dma_start(cell_list[:], offs)
        nc.sync.dma_start(out=words[:].bitcast(I32), in_=x_words[0].rearrange("p n t -> p (n t)").bitcast(I32))
        nc.sync.dma_start(out=old_sb[:], in_=old)
        nc.gpsimd.memset(wgt_rows[:], 0.0)
        nc.sync.dma_start(out=wgt_rows[0 : 2 * D, :], in_=wgt.rearrange("d p (h c) -> (d p h) c", h=2)[0 : 2 * D * P : P + 1, :])
        nc.sync.dma_start(out=vel_sb[:], in_=vel)
        for tile, lst in zip(corner, (cor1, cor2, cor3, cor4)):
            nc.sync.dma_start(tile[:], lst)

        w_bf = sb.tile([P, N, 4], BF16, name="w_bf", align_bytes=64)
        w_codes = sb.tile([P, N], U32, name="w_codes", align_bytes=64)
        w_scales = sb.tile([P, N], U8, name="w_scales", align_bytes=64)
        nc.scalar.activation(out=w_bf[:], in_=w_raw[:].rearrange("p j m -> p m j"), func=COPY)
        picked_scales = sb.tile([P, S], U8, name="picked_scales", align_bytes=64)
        nc.vector.tensor_copy(out=picked_scales[:], in_=scales[:].indirect(cell_list[:]))
        nc.vector.quantize_mx(out=w_codes[:].bitcast(FP8X4), scales=w_scales[:], in_=w_bf[:].rearrange("p m j -> p (m j)"))

        def turn(dst, src, start, stop):
            nc.tensor.matmul(dst, lhsT=src, rhs=ident[:], is_transpose=True, start=start, stop=stop)

        halves = [slice(h * P, (h + 1) * P) for h in range(2)]
        picked_words = sb.tile([P, S], U32, name="picked_words", align_bytes=64)
        y = sb.tile([P, S], F32, name="y")
        change = sb.tile([P, S], F32, name="change", tag="change_then_terms")
        banks = []
        for i, (a, b) in enumerate(PIECES):
            nc.vector.tensor_copy(out=picked_words[:, a:b], in_=words[:].indirect(cell_list[:, a // 16 : b // 16]))
            bank = ps.tile([P, S], F32, name=f"y_bank{i}")
            nc.tensor.matmul_mx(
                out=bank[:, 0 : b - a],
                lhsT=w_codes[:].bitcast(FP8X4),
                lhsT_scale=w_scales[:],
                rhs=picked_words[:, a:b].bitcast(FP8X4),
                rhs_scale=picked_scales[:, a:b],
                start=True,
                stop=True,
            )
            banks.append(bank)
        for bank, (a, b) in zip(banks, PIECES):
            nc.scalar.copy(out=y[:, a:b], in_=bank[:, 0 : b - a])
            nc.vector.tensor_tensor(out=change[:, a:b], in0=bank[:, 0 : b - a], in1=old_sb[:, a:b], op=ALU.subtract)

        turned = ps.tile([P, 4, P], F32, name="turned", tag="shared")
        turn(turned[:, 0, :], wgt_rows[:], True, True)
        for h in range(2):
            turn(turned[:, 2 + h, :], vel_sb[:, halves[h]], True, True)
        wgt_t = sb.tile([P, 2 * D], F32, name="wgt_t")
        vel_t = sb.tile([P, 2, P], F32, name="vel_t")
        nc.scalar.copy(out=wgt_t[:], in_=turned[:, 0, 0 : 2 * D])
        nc.scalar.copy(out=vel_t[:], in_=turned[:, 2:4, :])
        trial = ps.tile([P, 4, P], F32, name="trial", tag="shared")
        for h in range(2):
            turn(trial[:, h, :], vel_t[:, h, :], h == 0, False)

        g = sb.tile([P, D, U], F32, name="g")
        change_at = [sb.tile([P, U], F32, name=f"change_at{d}") for d in range(D)]
        change_t = [ps.tile([P, 4, P], F32, name=f"change_t{d}") for d in range(D)]
        for d in range(D):
            if d < D - 1:
                nc.scalar.activation(out=change_at[d][:], in_=change[:].indirect(corner[d][:]), func=COPY)
            else:
                nc.scalar.activation(out=change_at[d][:, halves[0]], in_=change[:].indirect(corner[d][:, 0 : P // 16]), func=COPY)
                nc.vector.tensor_copy(out=change_at[d][:, halves[1]], in_=change[:].indirect(corner[d][:, P // 16 : U // 16]))
            nc.vector.tensor_copy(out=g[:, d, :], in_=y[:].indirect(corner[d][:]))
            for h in range(2):
                turn(change_t[d][:, h, :], change_at[d][:, halves[h]], True, True)

        term_t = sb.tile([P, D, 2, P], F32, name="term_t", tag="change_then_terms")
        for d in range(D):
            for h in range(2):
                nc.scalar.activation(out=term_t[:, d, h, :], in_=change_t[d][:, h, :], func=COPY, scale=wgt_t[:, 2 * d + h : 2 * d + h + 1])
                turn(trial[:, h, :], term_t[:, d, h, :], False, d == D - 1 and h == 1)

        low2 = sb.tile([P, 2, U], F32, name="low2")
        high2 = sb.tile([P, 2, U], F32, name="high2")
        low = sb.tile([P, U], F32, name="low")
        high = sb.tile([P, U], F32, name="high")
        nc.vector.tensor_tensor(out=low2[:], in0=g[:, 0:2, :], in1=g[:, 2:4, :], op=ALU.min)
        nc.vector.tensor_tensor(out=high2[:], in0=g[:, 0:2, :], in1=g[:, 2:4, :], op=ALU.max)
        nc.vector.tensor_tensor(out=low[:], in0=low2[:, 0, :], in1=low2[:, 1, :], op=ALU.min)
        nc.vector.tensor_tensor(out=high[:], in0=high2[:, 0, :], in1=high2[:, 1, :], op=ALU.max)
        raised = sb.tile([P, U], F32, name="raised")
        result = sb.tile([P, U], F32, name="result")
        for h in range(2):
            nc.vector.tensor_tensor(out=raised[:, halves[h]], in0=trial[:, h, :], in1=low[:, halves[h]], op=ALU.max)
        for h, queue in enumerate((nc.sync, nc.scalar)):
            nc.vector.tensor_tensor(out=result[:, halves[h]], in0=raised[:, halves[h]], in1=high[:, halves[h]], op=ALU.min)
            queue.dma_start(out=out[:, halves[h]], in_=result[:, halves[h]])
